import numpy as np
import ml_dtypes


def mxq(x, axis, fmt="e4m3"):
    dtype, down = {"e4m3": (ml_dtypes.float8_e4m3fn, 7), "e5m2": (ml_dtypes.float8_e5m2, 14)}[fmt]
    v = np.moveaxis(np.asarray(x, np.float32).astype(ml_dtypes.bfloat16).astype(np.float64), axis, -1)
    blocks = v.reshape(v.shape[:-1] + (-1, 32))
    amax = np.abs(blocks).max(-1, keepdims=True)
    byte = np.maximum(np.where(amax > 0, np.frexp(amax)[1] - 1 + 127, 0) - down, 1)
    scale = np.exp2(byte - 127.0)
    codes = (blocks / scale).astype(np.float32).astype(dtype).astype(np.float64)
    return np.moveaxis((codes * scale).reshape(v.shape), -1, axis)


WIDE = False


def mx_kscale(k):
    if not WIDE:
        return np.ones(k)
    levels = np.array([10, -10, 5, -5, 0])
    if k % 512:
        return np.exp2(np.random.permutation(np.resize(levels, k // 32))).repeat(32)
    a = np.empty((k // 512, 16))
    for p in range(k // 512):
        a[p, :8] = np.random.permutation(np.resize(levels, 8))
        for g in range(8):
            far = levels[np.abs(levels - a[p, g]) >= 10]
            a[p, g + 8] = far[np.random.randint(len(far))]
    return np.exp2(a.ravel()).repeat(32)


def f64(x):
    return np.asarray(x).astype(np.float64)


def striped(idx):
    return np.tile(np.asarray(idx).reshape(-1, 16).T, (8, 1)).astype(np.uint16)


def unstriped(offs):
    return offs[:16].T.reshape(-1).astype(np.int64)


E2M1 = np.array([0.0, 0.5, 1.0, 1.5, 2.0, 3.0, 4.0, 6.0, -0.0, -0.5, -1.0, -1.5, -2.0, -3.0, -4.0, -6.0])


def pack_weight(w, fmt):
    k, n = w.shape
    w = f64(np.asarray(w, np.float32).astype(ml_dtypes.bfloat16)).reshape(k // 32, 32, n)
    amax = np.abs(w).max(1)
    if fmt == "e4m3":
        byte = np.frexp(amax)[1] - 1 + 127 - 7
    else:
        mant, ex = np.frexp(amax / 6.0)
        byte = np.where(mant > 0.5, ex, ex - 1) + 127
    byte = np.clip(np.where(amax > 0, byte, 1), 1, 254)
    scaled = (w * np.exp2(127.0 - byte)[:, None, :]).reshape(k, n).astype(np.float32)
    by_word = np.ascontiguousarray(scaled.reshape(k // 512, 128, 4, n).transpose(0, 1, 3, 2))
    if fmt == "e4m3":
        words = by_word.astype(ml_dtypes.float8_e4m3fn).view(np.uint8)
    else:
        c = by_word.astype(ml_dtypes.float4_e2m1fn).view(np.uint8) & 0xF
        words = (c[..., 0::2] | (c[..., 1::2] << 4)).reshape(k // 512, 128, 2 * n)
    return np.ascontiguousarray(words), np.ascontiguousarray(byte.astype(np.uint8).reshape(k // 512, 16, n))


def unpack_weight(words, scales, fmt):
    g, _, n = scales.shape
    words = np.ascontiguousarray(words).reshape(g, 128, n, -1)
    if fmt == "e4m3":
        vals = words.view(ml_dtypes.float8_e4m3fn).astype(np.float64)
    else:
        nib = np.empty((g, 128, n, 4), np.uint8)
        nib[..., 0::2] = words & 0xF
        nib[..., 1::2] = words >> 4
        vals = E2M1[nib]
    vals = vals * np.repeat(np.exp2(scales.astype(np.float64) - 127.0), 8, axis=1)[..., None]
    return vals.transpose(0, 1, 3, 2).reshape(g * 512, n)


def sigmoid(v):
    return 1.0 / (1.0 + np.exp(-v))


def bf(x):
    return np.asarray(x, np.float32).astype(ml_dtypes.bfloat16)


def planes(Y):
    r, m = Y.shape
    b = f64(bf(Y)).reshape(r // 32, 32, m)
    amax = np.abs(b).max(1)
    byte = np.clip(np.where(amax > 0, np.frexp(amax)[1] - 1 + 127 - 7, 1), 1, 254)
    codes = (b * np.exp2(127.0 - byte)[:, None, :]).reshape(r, m).astype(np.float32).astype(ml_dtypes.float8_e4m3fn).view(np.uint8)
    words = codes.reshape(r // 512, 128, 4, m).transpose(0, 1, 3, 2)
    return np.ascontiguousarray(words), np.ascontiguousarray(byte.astype(np.uint8).reshape(r // 512, 16, m))


D, T, I, Q, E = 512, 2048, 512, 256, 512


def setup_inputs():
    n = np.random.standard_normal
    idx = np.random.permutation(T)[:I]
    fd = mx_kscale(D)
    fi = mx_kscale(I)
    ti = np.ones(T)
    ti[idx] = fi
    keysp = pack_weight(n((D, T)) / fd[:, None], "e2m1")
    return {
        "query": (n((D, Q)) * 0.8 / np.sqrt(D) * fd[:, None]).astype(np.float32),
        "query2": (n((D, Q)) * 0.8 / np.sqrt(D) * fd[:, None]).astype(np.float32),
        "keys_words": keysp[0],
        "keys_scales": keysp[1],
        "ba": (np.random.uniform(-1.0, 0.5, (Q, 1))).astype(np.float32),
        "bb": (np.random.uniform(-1.0, 0.5, (Q, 1))).astype(np.float32),
        "size": (np.random.uniform(0.5, 2.0, (1, I)) * fi).astype(np.float32),
        "vals": (n((E, T)) / ti).astype(np.float32),
        "offs": striped(idx),
    }


def reference(query, query2, keys_words, keys_scales, ba, bb, size, vals, offs):
    idx = unstriped(offs)
    keysu = unpack_weight(keys_words, keys_scales, "e2m1")
    queryq = mxq(f64(query), 0, "e4m3")
    keysidxg = keysu[:, idx]
    a = queryq.T @ keysidxg
    query2q = mxq(f64(query2), 0, "e4m3")
    b = query2q.T @ keysidxg
    p = sigmoid(a + f64(ba)) * sigmoid(b + f64(bb))
    w = p * f64(size) / np.sum(p, axis=1, keepdims=True)
    wt = w.T
    vt = f64(vals)[:, idx].T
    vtq = mxq(vt, 0, "e4m3")
    wtq = mxq(wt, 0, "e4m3")
    o = vtq.T @ wtq
    words, scales = planes(o)
    return o, words, scales

@@ -1,0 +1,211 @@
+from contextlib import ExitStack
+
+import concourse.mybir as mybir
+
+D, T, I, Q, E = 512, 2048, 512, 256, 512
+FLOPS = 2 * D * Q * I * 2 + 2 * I * E * Q
+
+F32 = mybir.dt.float32
+BF16 = mybir.dt.bfloat16
+I32 = mybir.dt.int32
+U32 = mybir.dt.uint32
+U16 = mybir.dt.uint16
+U8 = mybir.dt.uint8
+FP8X4 = mybir.dt.float8_e4m3fn_x4
+FP4X4 = mybir.dt.float4_e2m1fn_x4
+MULT = mybir.AluOpType.mult
+COPY = mybir.ActivationFunctionType.Copy
+SIGMOID = mybir.ActivationFunctionType.Sigmoid
+
+P = 128
+PACK = 4
+HALVES = Q // P
+BANK = 512
+
+
+def tile_attend_bothquestions_pl_kernel(
+    tc, query, query2, keys_words, keys_scales, ba, bb, size, vals, offs, out_0, out_1, out_2
+):
+    nc = tc.nc
+    with ExitStack() as ctx:
+        sb = ctx.enter_context(tc.tile_pool(name="sb", bufs=1))
+        psum = ctx.enter_context(tc.psum_pool(name="psum", bufs=1))
+
+        def bank(k, name):
+            return psum.tile([P, BANK], F32, name=name, tag="bank%d" % k)
+
+        def mx_tiles(name, width):
+            codes = sb.tile([P, width], U32, name=name + "_codes", align_bytes=64)
+            scales = sb.tile([P, width], U8, name=name + "_scales", align_bytes=64)
+            return codes, scales
+
+        offsets = sb.tile([P, I // 16], U16, name="offsets")
+        nc.sync.dma_start(offsets[:], offs)
+
+        key_scale_pool = sb.tile([P, T], U8, name="key_scale_pool")
+        nc.vector.memset(key_scale_pool[:].bitcast(I32), 0)
+        for quad in range(4):
+            nc.scalar.dma_start(
+                key_scale_pool[32 * quad : 32 * quad + 4, :].bitcast(I32),
+                keys_scales[0, 4 * quad : 4 * quad + 4, :].bitcast(I32),
+            )
+        ident = sb.tile([P, P], F32, name="ident")
+        ones = sb.tile([P, P], F32, name="ones", tag="vec_rows")
+        nc.gpsimd.memset(ones[:], 1.0)
+        nc.gpsimd.affine_select(
+            out=ident[:],
+            in_=ones[:],
+            compare_op=mybir.AluOpType.is_equal,
+            fill=0.0,
+            base=0,
+            pattern=[[-1, P]],
+            channel_multiplier=1,
+        )
+
+        vec_rows = sb.tile([P, P], F32, name="vec_rows")
+        nc.gpsimd.memset(vec_rows[:], 0.0)
+        nc.gpsimd.dma_start(vec_rows[0:2, :], ba.rearrange("(h p) o -> h (p o)", p=P))
+        nc.gpsimd.dma_start(vec_rows[2:4, :], bb.rearrange("(h p) o -> h (p o)", p=P))
+        nc.gpsimd.dma_start(vec_rows[4:8, :], size.rearrange("o (c p) -> (o c) p", p=P))
+
+        key_word_pool = sb.tile([P, T], U16, name="key_word_pool", tag="ring1")
+        nc.sync.dma_start(key_word_pool[:].bitcast(I32), keys_words[0].bitcast(I32))
+
+        q_raw = []
+        for n, src in enumerate((query, query2)):
+            raw = sb.tile([P, PACK, Q], F32, name="q_raw%d" % n, tag="ring%d" % (2 + n))
+            nc.sync.dma_start(raw[:], src.rearrange("(p j) q -> p j q", j=PACK))
+            q_raw.append(raw)
+
+        vals_rows = vals.rearrange("(m j) t -> j m t", j=PACK)
+        val_pools = []
+
+        def load_values(j):
+            pool_j = sb.tile([P, T], F32, name="val_pool%d" % j, tag="ring%d" % j)
+            nc.sync.dma_start(pool_j[:], vals_rows[j])
+            val_pools.append(pool_j)
+
+        load_values(0)
+
+        key_words = sb.tile([P, I], U16, name="key_words", align_bytes=64)
+        nc.vector.tensor_copy(key_words[:], key_word_pool[:].indirect(offsets[:]))
+
+        key_scales = sb.tile([P, I], U8, name="key_scales", align_bytes=64)
+        nc.vector.tensor_copy(key_scales[:], key_scale_pool[:].indirect(offsets[:]))
+
+        vec_bank = bank(7, "vec_bank")
+        nc.tensor.transpose(vec_bank[:, :P], vec_rows[:], ident[:])
+        vec_cols = sb.tile([P, 8], F32, name="vec_cols", tag="picked1", align_bytes=64)
+        nc.vector.tensor_copy(vec_cols[:], vec_bank[:, :8])
+        size_bank = bank(0, "size_bank")
+        for c in range(I // P):
+            nc.tensor.transpose(
+                size_bank[:, c * P : (c + 1) * P], vec_cols[:, 4 + c : 5 + c].to_broadcast([P, P]), ident[:]
+            )
+
+        sig = {}
+        for n in range(2):
+            grouped = sb.tile([P, Q, PACK], BF16, name="q_grouped%d" % n, tag=("q_grouped0", "picked0")[n], align_bytes=64)
+            nc.vector.tensor_copy(
+                grouped[:].rearrange("p (c i) j -> p c j i", i=4),
+                q_raw[n][:].rearrange("p j (c i) -> p c j i", i=4),
+            )
+            codes, scales = mx_tiles("q%d" % n, Q)
+            nc.vector.quantize_mx(codes[:].bitcast(FP8X4), scales[:], grouped[:].rearrange("p q j -> p (q j)"))
+            for h in range(HALVES):
+                cols = slice(h * P, (h + 1) * P)
+                scores = bank(3 + 2 * n + h, "scores%d%d" % (n, h))
+                nc.tensor.matmul_mx(
+                    scores[:],
+                    lhsT=codes[:, cols].bitcast(FP8X4),
+                    lhsT_scale=scales[:, cols],
+                    rhs=key_words[:].bitcast(FP4X4),
+                    rhs_scale=key_scales[:],
+                    start=True,
+                    stop=True,
+                )
+                sig[n, h] = sb.tile([P, I], F32, name="sig%d%d" % (n, h))
+                nc.scalar.activation(sig[n, h][:], scores[:], SIGMOID, bias=vec_cols[:, 2 * n + h : 2 * n + h + 1])
+
+        for j in range(1, PACK):
+            load_values(j)
+
+        def turn_and_quantise(name, rows, turn_bank):
+            words = rows[:].bitcast(F32)
+            turned = bank(turn_bank, name + "_turned")
+            for u in range(2):
+                nc.tensor.transpose(turned[:, u * P : (u + 1) * P], words[:, u : I // 2 : 2], ident[:])
+            grouped = sb.tile([P, P * PACK], BF16, name=name + "_grouped", align_bytes=64)
+            nc.scalar.copy(
+                grouped[:].bitcast(F32).rearrange("p (c u) -> p c u", u=2),
+                turned[:, : 2 * P].rearrange("p (u c) -> p c u", u=2),
+            )
+            codes, scales = mx_tiles(name, P)
+            nc.vector.quantize_mx(codes[:].bitcast(FP8X4), scales[:], grouped[:])
+            return codes, scales
+
+        def values(j, on_vector, turn_bank):
+            picked = sb.tile([P, I], BF16, name="picked%d" % j, tag="picked%d" % min(j, 2), align_bytes=64)
+            if on_vector > 0:
+                nc.vector.tensor_copy(picked[:, :on_vector], val_pools[j][:].indirect(offsets[:, : on_vector // 16]))
+            if on_vector < I:
+                nc.scalar.activation(picked[:, on_vector:], val_pools[j][:].indirect(offsets[:, on_vector // 16 :]), COPY)
+            return turn_and_quantise("v%d" % j, picked, turn_bank)
+
+        def weights(h, turn_bank):
+            p = sb.tile([P, I], F32, name="p%d" % h, tag=("p0", "picked2")[h], align_bytes=64)
+            total = sb.tile([P, 1], F32, name="total%d" % h)
+            nc.vector.scalar_tensor_tensor(p[:], sig[0, h][:], 1.0, sig[1, h][:], MULT, MULT, accum_out=total[:])
+            inverse = sb.tile([P, 1], F32, name="inverse%d" % h)
+            nc.vector.reciprocal(inverse[:], total[:])
+            w = sb.tile([P, I], BF16, name="w%d" % h)
+            nc.vector.scalar_tensor_tensor(w[:], p[:], inverse[:], size_bank[:], MULT, MULT)
+            return turn_and_quantise("w%d" % h, w, turn_bank)
+
+        v_mx = {0: values(0, I, 7)}
+        w_mx = [weights(0, 3), weights(1, 4)]
+        v_mx[1] = values(1, 0, 5)
+        v_mx[2] = values(2, I // 2, 6)
+
+        result = [bank(1 + h, "result%d" % h) for h in range(HALVES)]
+
+        def multiply(j):
+            for h in range(HALVES):
+                nc.tensor.matmul_mx(
+                    result[h][:, j * P : (j + 1) * P],
+                    lhsT=v_mx[j][0][:].bitcast(FP8X4),
+                    lhsT_scale=v_mx[j][1][:],
+                    rhs=w_mx[h][0][:].bitcast(FP8X4),
+                    rhs_scale=w_mx[h][1][:],
+                    start=True,
+                    stop=True,
+                )
+
+        out_rows = out_0.rearrange("(p j) q -> p j q", j=PACK)
+        last = PACK - 1
+        v_mx[last] = values(last, I // 2, 7)
+        for j in range(last):
+            multiply(j)
+            rows = sb.tile([P, Q], F32, name="rows%d" % j)
+            nc.vector.tensor_copy(rows[:, :P], result[0][:, j * P : (j + 1) * P])
+            nc.scalar.copy(rows[:, P:], result[1][:, j * P : (j + 1) * P])
+            nc.sync.dma_start(out_rows[:, j, :], rows[:])
+
+        multiply(last)
+        y_grouped = sb.tile([P, Q, PACK], BF16, name="y_grouped", align_bytes=64)
+        nc.vector.tensor_copy(y_grouped[:, :P, :], result[0][:].rearrange("p (j q) -> p q j", j=PACK))
+        nc.scalar.copy(y_grouped[:, P:, :], result[1][:].rearrange("p (j q) -> p q j", j=PACK))
+        late = sb.tile([P, Q], F32, name="late")
+        for h in range(HALVES):
+            nc.scalar.copy(late[:, h * P : (h + 1) * P], result[h][:, last * P :])
+        nc.scalar.dma_start(out_rows[:, last, :], late[:])
+
+        y_codes, y_scales = mx_tiles("y", Q)
+        nc.vector.quantize_mx(y_codes[:].bitcast(FP8X4), y_scales[:], y_grouped[:].rearrange("p q j -> p (q j)"))
+        nc.sync.dma_start(out_1[0].rearrange("p c r -> p (c r)").bitcast(I32), y_codes[:].bitcast(I32))
+        for quad in range(4):
+            queue = nc.sync if quad % 2 == 0 else nc.scalar
+            queue.dma_start(
+                out_2[0, 4 * quad : 4 * quad + 4, :].bitcast(I32),
+                y_scales[32 * quad : 32 * quad + 4, :].bitcast(I32),
+            )

@@ -43,14 +43,14 @@ def tile_attend_bothquestions_pl_kernel(
         nc.sync.dma_start(offsets[:], offs)
 
         key_scale_pool = sb.tile([P, T], U8, name="key_scale_pool")
-        nc.vector.memset(key_scale_pool[:].bitcast(I32), 0)
+        nc.gpsimd.memset(key_scale_pool[:].bitcast(I32), 0)
         for quad in range(4):
             nc.scalar.dma_start(
                 key_scale_pool[32 * quad : 32 * quad + 4, :].bitcast(I32),
                 keys_scales[0, 4 * quad : 4 * quad + 4, :].bitcast(I32),
             )
         ident = sb.tile([P, P], F32, name="ident")
-        ones = sb.tile([P, P], F32, name="ones", tag="vec_rows")
+        ones = sb.tile([P, P], F32, name="ones", tag="ring0")
         nc.gpsimd.memset(ones[:], 1.0)
         nc.gpsimd.affine_select(
             out=ident[:],
@@ -62,12 +62,15 @@ def tile_attend_bothquestions_pl_kernel(
             channel_multiplier=1,
         )
 
-        vec_rows = sb.tile([P, P], F32, name="vec_rows")
-        nc.gpsimd.memset(vec_rows[:], 0.0)
-        nc.gpsimd.dma_start(vec_rows[0:2, :], ba.rearrange("(h p) o -> h (p o)", p=P))
-        nc.gpsimd.dma_start(vec_rows[2:4, :], bb.rearrange("(h p) o -> h (p o)", p=P))
-        nc.gpsimd.dma_start(vec_rows[4:8, :], size.rearrange("o (c p) -> (o c) p", p=P))
+        size_cols = sb.tile([P, PACK], F32, name="size_cols")
+        nc.sync.dma_start(size_cols[:], size.rearrange("o (p t) -> p (o t)", t=PACK))
 
+        biases = []
+        for n, src in enumerate((ba, bb)):
+            bias = sb.tile([P, HALVES], F32, name="bias%d" % n, tag=("bias0", "picked1")[n], align_bytes=64)
+            with nc.allow_non_contiguous_dma(reason="one bias value a partition for each half of the query rows"):
+                nc.sync.dma_start(bias[:], src.rearrange("(h p) o -> p (h o)", p=P))
+            biases.append(bias)
         key_word_pool = sb.tile([P, T], U16, name="key_word_pool", tag="ring1")
         nc.sync.dma_start(key_word_pool[:].bitcast(I32), keys_words[0].bitcast(I32))
 
@@ -93,28 +96,29 @@ def tile_attend_bothquestions_pl_kernel(
         key_scales = sb.tile([P, I], U8, name="key_scales", align_bytes=64)
         nc.vector.tensor_copy(key_scales[:], key_scale_pool[:].indirect(offsets[:]))
 
-        vec_bank = bank(7, "vec_bank")
-        nc.tensor.transpose(vec_bank[:, :P], vec_rows[:], ident[:])
-        vec_cols = sb.tile([P, 8], F32, name="vec_cols", tag="picked1", align_bytes=64)
-        nc.vector.tensor_copy(vec_cols[:], vec_bank[:, :8])
         size_bank = bank(0, "size_bank")
-        for c in range(I // P):
+        for t in range(PACK):
             nc.tensor.transpose(
-                size_bank[:, c * P : (c + 1) * P], vec_cols[:, 4 + c : 5 + c].to_broadcast([P, P]), ident[:]
+                size_bank[:, t * P : (t + 1) * P], size_cols[:, t : t + 1].to_broadcast([P, P]), ident[:]
             )
+        size_rows = size_bank[:].rearrange("q (t p) -> q p t", t=PACK)
 
         sig = {}
+        q_mx = []
         for n in range(2):
             grouped = sb.tile([P, Q, PACK], BF16, name="q_grouped%d" % n, tag=("q_grouped0", "picked0")[n], align_bytes=64)
-            nc.vector.tensor_copy(
+            (nc.scalar.copy, nc.vector.tensor_copy)[n](
                 grouped[:].rearrange("p (c i) j -> p c j i", i=4),
                 q_raw[n][:].rearrange("p j (c i) -> p c j i", i=4),
             )
             codes, scales = mx_tiles("q%d" % n, Q)
             nc.vector.quantize_mx(codes[:].bitcast(FP8X4), scales[:], grouped[:].rearrange("p q j -> p (q j)"))
-            for h in range(HALVES):
-                cols = slice(h * P, (h + 1) * P)
-                scores = bank(3 + 2 * n + h, "scores%d%d" % (n, h))
+            q_mx.append((codes, scales))
+        for h in range(HALVES):
+            cols = slice(h * P, (h + 1) * P)
+            for n in range(2):
+                codes, scales = q_mx[n]
+                scores = bank(3 + n, "scores%d%d" % (n, h))
                 nc.tensor.matmul_mx(
                     scores[:],
                     lhsT=codes[:, cols].bitcast(FP8X4),
@@ -125,7 +129,7 @@ def tile_attend_bothquestions_pl_kernel(
                     stop=True,
                 )
                 sig[n, h] = sb.tile([P, I], F32, name="sig%d%d" % (n, h))
-                nc.scalar.activation(sig[n, h][:], scores[:], SIGMOID, bias=vec_cols[:, 2 * n + h : 2 * n + h + 1])
+                nc.scalar.activation(sig[n, h][:], scores[:], SIGMOID, bias=biases[n][:, h : h + 1])
 
         for j in range(1, PACK):
             load_values(j)
@@ -135,7 +139,7 @@ def tile_attend_bothquestions_pl_kernel(
             turned = bank(turn_bank, name + "_turned")
             for u in range(2):
                 nc.tensor.transpose(turned[:, u * P : (u + 1) * P], words[:, u : I // 2 : 2], ident[:])
-            grouped = sb.tile([P, P * PACK], BF16, name=name + "_grouped", align_bytes=64)
+            grouped = sb.tile([P, P * PACK], BF16, name=name + "_grouped", tag=name + "_grouped", align_bytes=64)
             nc.scalar.copy(
                 grouped[:].bitcast(F32).rearrange("p (c u) -> p c u", u=2),
                 turned[:, : 2 * P].rearrange("p (u c) -> p c u", u=2),
@@ -159,13 +163,20 @@ def tile_attend_bothquestions_pl_kernel(
             inverse = sb.tile([P, 1], F32, name="inverse%d" % h)
             nc.vector.reciprocal(inverse[:], total[:])
             w = sb.tile([P, I], BF16, name="w%d" % h)
-            nc.vector.scalar_tensor_tensor(w[:], p[:], inverse[:], size_bank[:], MULT, MULT)
+            nc.vector.scalar_tensor_tensor(
+                w[:].rearrange("q (p t) -> q p t", t=PACK),
+                p[:].rearrange("q (p t) -> q p t", t=PACK),
+                inverse[:],
+                size_rows,
+                MULT,
+                MULT,
+            )
             return turn_and_quantise("w%d" % h, w, turn_bank)
 
         v_mx = {0: values(0, I, 7)}
-        w_mx = [weights(0, 3), weights(1, 4)]
-        v_mx[1] = values(1, 0, 5)
-        v_mx[2] = values(2, I // 2, 6)
+        w_mx = [weights(0, 5), weights(1, 3)]
+        v_mx[1] = values(1, 0, 6)
+        v_mx[2] = values(2, I // 2, 4)
 
         result = [bank(1 + h, "result%d" % h) for h in range(HALVES)]
 
@@ -183,13 +194,13 @@ def tile_attend_bothquestions_pl_kernel(
 
         out_rows = out_0.rearrange("(p j) q -> p j q", j=PACK)
         last = PACK - 1
-        v_mx[last] = values(last, I // 2, 7)
         for j in range(last):
             multiply(j)
-            rows = sb.tile([P, Q], F32, name="rows%d" % j)
-            nc.vector.tensor_copy(rows[:, :P], result[0][:, j * P : (j + 1) * P])
-            nc.scalar.copy(rows[:, P:], result[1][:, j * P : (j + 1) * P])
-            nc.sync.dma_start(out_rows[:, j, :], rows[:])
+        v_mx[last] = values(last, I // 2, 7)
+        early = sb.tile([P, last, Q], F32, name="early", tag="ring%d" % last)
+        nc.scalar.copy(early[:, :, :P], result[0][:, : last * P].rearrange("p (j q) -> p j q", j=last))
+        nc.scalar.copy(early[:, :, P:], result[1][:, : last * P].rearrange("p (j q) -> p j q", j=last))
+        nc.sync.dma_start(out_rows[:, :last, :], early[:])
 
         multiply(last)
         y_grouped = sb.tile([P, Q, PACK], BF16, name="y_grouped", align_bytes=64)

@@ -1,6 +1,7 @@
 from contextlib import ExitStack
 
 import concourse.mybir as mybir
+from concourse.masks import make_identity
 
 D, T, I, Q, E = 512, 2048, 512, 256, 512
 FLOPS = 2 * D * Q * I * 2 + 2 * I * E * Q
@@ -21,6 +22,7 @@ P = 128
 PACK = 4
 HALVES = Q // P
 BANK = 512
+Y_SPLIT = 168
 
 
 def tile_attend_bothquestions_pl_kernel(
@@ -34,61 +36,55 @@ def tile_attend_bothquestions_pl_kernel(
         def bank(k, name):
             return psum.tile([P, BANK], F32, name=name, tag="bank%d" % k)
 
-        def mx_tiles(name, width):
-            codes = sb.tile([P, width], U32, name=name + "_codes", align_bytes=64)
+        def mx_tiles(name, width, tag=None):
+            codes = sb.tile([P, width], U32, name=name + "_codes", tag=tag or name + "_codes", align_bytes=64)
             scales = sb.tile([P, width], U8, name=name + "_scales", align_bytes=64)
             return codes, scales
 
         offsets = sb.tile([P, I // 16], U16, name="offsets")
         nc.sync.dma_start(offsets[:], offs)
 
+        warm_in = sb.tile([P, 1], F32, name="warm_in")
+        warm_out = sb.tile([P, 1], F32, name="warm_out")
+        nc.vector.memset(warm_in[:], 0.0)
+        nc.scalar.activation(warm_out[:], warm_in[:], SIGMOID)
+
         key_scale_pool = sb.tile([P, T], U8, name="key_scale_pool")
-        nc.gpsimd.memset(key_scale_pool[:].bitcast(I32), 0)
+        nc.vector.memset(key_scale_pool[:].bitcast(I32), 0)
         for quad in range(4):
             nc.scalar.dma_start(
                 key_scale_pool[32 * quad : 32 * quad + 4, :].bitcast(I32),
                 keys_scales[0, 4 * quad : 4 * quad + 4, :].bitcast(I32),
             )
         ident = sb.tile([P, P], F32, name="ident")
-        ones = sb.tile([P, P], F32, name="ones", tag="ring0")
-        nc.gpsimd.memset(ones[:], 1.0)
-        nc.gpsimd.affine_select(
-            out=ident[:],
-            in_=ones[:],
-            compare_op=mybir.AluOpType.is_equal,
-            fill=0.0,
-            base=0,
-            pattern=[[-1, P]],
-            channel_multiplier=1,
-        )
+        make_identity(nc, ident[:])
 
-        size_cols = sb.tile([P, PACK], F32, name="size_cols")
-        nc.sync.dma_start(size_cols[:], size.rearrange("o (p t) -> p (o t)", t=PACK))
-
-        biases = []
-        for n, src in enumerate((ba, bb)):
+        def load_bias(n, src):
             bias = sb.tile([P, HALVES], F32, name="bias%d" % n, tag=("bias0", "picked1")[n], align_bytes=64)
             with nc.allow_non_contiguous_dma(reason="one bias value a partition for each half of the query rows"):
                 nc.sync.dma_start(bias[:], src.rearrange("(h p) o -> p (h o)", p=P))
-            biases.append(bias)
-        key_word_pool = sb.tile([P, T], U16, name="key_word_pool", tag="ring1")
-        nc.sync.dma_start(key_word_pool[:].bitcast(I32), keys_words[0].bitcast(I32))
+            return bias
 
-        q_raw = []
-        for n, src in enumerate((query, query2)):
-            raw = sb.tile([P, PACK, Q], F32, name="q_raw%d" % n, tag="ring%d" % (2 + n))
+        def load_query(n, src):
+            raw = sb.tile([P, PACK, Q], F32, name="q_raw%d" % n, tag=("ring0", "sig00")[n], align_bytes=64)
             nc.sync.dma_start(raw[:], src.rearrange("(p j) q -> p j q", j=PACK))
-            q_raw.append(raw)
+            return raw
+
+        size_cols = sb.tile([P, PACK], F32, name="size_cols")
+        nc.sync.dma_start(size_cols[:], size.rearrange("o (p t) -> p (o t)", t=PACK))
+        biases = [load_bias(0, ba), load_bias(1, bb)]
+        q_raw = [load_query(0, query)]
+        key_word_pool = sb.tile([P, T], U16, name="key_word_pool")
+        nc.sync.dma_start(key_word_pool[:].bitcast(I32), keys_words[0].bitcast(I32))
+        q_raw.append(load_query(1, query2))
 
         vals_rows = vals.rearrange("(m j) t -> j m t", j=PACK)
         val_pools = []
 
         def load_values(j):
-            pool_j = sb.tile([P, T], F32, name="val_pool%d" % j, tag="ring%d" % j)
+            pool_j = sb.tile([P, T], F32, name="val_pool%d" % j, tag="ring%d" % j, align_bytes=64)
             nc.sync.dma_start(pool_j[:], vals_rows[j])
             val_pools.append(pool_j)
-
-        load_values(0)
 
         key_words = sb.tile([P, I], U16, name="key_words", align_bytes=64)
         nc.vector.tensor_copy(key_words[:], key_word_pool[:].indirect(offsets[:]))
@@ -96,24 +92,34 @@ def tile_attend_bothquestions_pl_kernel(
         key_scales = sb.tile([P, I], U8, name="key_scales", align_bytes=64)
         nc.vector.tensor_copy(key_scales[:], key_scale_pool[:].indirect(offsets[:]))
 
-        size_bank = bank(0, "size_bank")
+        size_bank = bank(3, "size_bank")
         for t in range(PACK):
             nc.tensor.transpose(
                 size_bank[:, t * P : (t + 1) * P], size_cols[:, t : t + 1].to_broadcast([P, P]), ident[:]
             )
-        size_rows = size_bank[:].rearrange("q (t p) -> q p t", t=PACK)
+        size_rows = sb.tile([P, I], F32, name="size_rows")
+        nc.scalar.copy(
+            size_rows[:].rearrange("q (p t) -> q p t", t=PACK), size_bank[:].rearrange("q (t p) -> q p t", t=PACK)
+        )
 
         sig = {}
-        q_mx = []
-        for n in range(2):
-            grouped = sb.tile([P, Q, PACK], BF16, name="q_grouped%d" % n, tag=("q_grouped0", "picked0")[n], align_bytes=64)
-            (nc.scalar.copy, nc.vector.tensor_copy)[n](
+        q_mx = [mx_tiles("q0", Q, "ring3"), mx_tiles("q1", Q)]
+
+        def quantise_query(n, cols, copy, tag):
+            width = cols.stop - cols.start
+            grouped = sb.tile([P, width, PACK], BF16, name="q_grouped_" + tag, tag=tag, align_bytes=64)
+            copy(
                 grouped[:].rearrange("p (c i) j -> p c j i", i=4),
-                q_raw[n][:].rearrange("p j (c i) -> p c j i", i=4),
+                q_raw[n][:, :, cols].rearrange("p j (c i) -> p c j i", i=4),
             )
-            codes, scales = mx_tiles("q%d" % n, Q)
-            nc.vector.quantize_mx(codes[:].bitcast(FP8X4), scales[:], grouped[:].rearrange("p q j -> p (q j)"))
-            q_mx.append((codes, scales))
+            codes, scales = q_mx[n]
+            nc.vector.quantize_mx(
+                codes[:, cols].bitcast(FP8X4), scales[:, cols], grouped[:].rearrange("p q j -> p (q j)")
+            )
+
+        quantise_query(0, slice(0, Q), nc.vector.tensor_copy, "ring1")
+        quantise_query(1, slice(0, P), nc.scalar.copy, "ring2")
+        quantise_query(1, slice(P, Q), nc.scalar.copy, "picked0")
         for h in range(HALVES):
             cols = slice(h * P, (h + 1) * P)
             for n in range(2):
@@ -128,13 +134,13 @@ def tile_attend_bothquestions_pl_kernel(
                     start=True,
                     stop=True,
                 )
-                sig[n, h] = sb.tile([P, I], F32, name="sig%d%d" % (n, h))
+                sig[n, h] = sb.tile([P, I], F32, name="sig%d%d" % (n, h), tag="sig%d%d" % (n, h), align_bytes=64)
                 nc.scalar.activation(sig[n, h][:], scores[:], SIGMOID, bias=biases[n][:, h : h + 1])
 
-        for j in range(1, PACK):
+        for j in range(PACK):
             load_values(j)
 
-        def turn_and_quantise(name, rows, turn_bank):
+        def turn_and_quantise(name, rows, turn_bank, codes, scales):
             words = rows[:].bitcast(F32)
             turned = bank(turn_bank, name + "_turned")
             for u in range(2):
@@ -144,9 +150,7 @@ def tile_attend_bothquestions_pl_kernel(
                 grouped[:].bitcast(F32).rearrange("p (c u) -> p c u", u=2),
                 turned[:, : 2 * P].rearrange("p (u c) -> p c u", u=2),
             )
-            codes, scales = mx_tiles(name, P)
-            nc.vector.quantize_mx(codes[:].bitcast(FP8X4), scales[:], grouped[:])
-            return codes, scales
+            nc.vector.quantize_mx(codes.bitcast(FP8X4), scales, grouped[:])
 
         def values(j, on_vector, turn_bank):
             picked = sb.tile([P, I], BF16, name="picked%d" % j, tag="picked%d" % min(j, 2), align_bytes=64)
@@ -154,7 +158,11 @@ def tile_attend_bothquestions_pl_kernel(
                 nc.vector.tensor_copy(picked[:, :on_vector], val_pools[j][:].indirect(offsets[:, : on_vector // 16]))
             if on_vector < I:
                 nc.scalar.activation(picked[:, on_vector:], val_pools[j][:].indirect(offsets[:, on_vector // 16 :]), COPY)
-            return turn_and_quantise("v%d" % j, picked, turn_bank)
+            codes, scales = mx_tiles("v%d" % j, P)
+            turn_and_quantise("v%d" % j, picked, turn_bank, codes[:], scales[:])
+            return codes, scales
+
+        w_codes, w_scales = mx_tiles("w", Q)
 
         def weights(h, turn_bank):
             p = sb.tile([P, I], F32, name="p%d" % h, tag=("p0", "picked2")[h], align_bytes=64)
@@ -163,53 +171,46 @@ def tile_attend_bothquestions_pl_kernel(
             inverse = sb.tile([P, 1], F32, name="inverse%d" % h)
             nc.vector.reciprocal(inverse[:], total[:])
             w = sb.tile([P, I], BF16, name="w%d" % h)
-            nc.vector.scalar_tensor_tensor(
-                w[:].rearrange("q (p t) -> q p t", t=PACK),
-                p[:].rearrange("q (p t) -> q p t", t=PACK),
-                inverse[:],
-                size_rows,
-                MULT,
-                MULT,
-            )
-            return turn_and_quantise("w%d" % h, w, turn_bank)
+            nc.vector.scalar_tensor_tensor(w[:], p[:], inverse[:], size_rows[:], MULT, MULT)
+            cols = slice(h * P, (h + 1) * P)
+            turn_and_quantise("w%d" % h, w, turn_bank, w_codes[:, cols], w_scales[:, cols])
+            return w
 
         v_mx = {0: values(0, I, 7)}
         w_mx = [weights(0, 5), weights(1, 3)]
         v_mx[1] = values(1, 0, 6)
         v_mx[2] = values(2, I // 2, 4)
 
-        result = [bank(1 + h, "result%d" % h) for h in range(HALVES)]
-
-        def multiply(j):
-            for h in range(HALVES):
-                nc.tensor.matmul_mx(
-                    result[h][:, j * P : (j + 1) * P],
-                    lhsT=v_mx[j][0][:].bitcast(FP8X4),
-                    lhsT_scale=v_mx[j][1][:],
-                    rhs=w_mx[h][0][:].bitcast(FP8X4),
-                    rhs_scale=w_mx[h][1][:],
-                    start=True,
-                    stop=True,
-                )
+        def multiply(j, result_bank):
+            result = bank(result_bank, "result%d" % j)
+            nc.tensor.matmul_mx(
+                result[:, :Q],
+                lhsT=v_mx[j][0][:].bitcast(FP8X4),
+                lhsT_scale=v_mx[j][1][:],
+                rhs=w_codes[:].bitcast(FP8X4),
+                rhs_scale=w_scales[:],
+                start=True,
+                stop=True,
+            )
+            return result
 
         out_rows = out_0.rearrange("(p j) q -> p j q", j=PACK)
         last = PACK - 1
-        for j in range(last):
-            multiply(j)
+        results = [multiply(j, j) for j in range(last)]
         v_mx[last] = values(last, I // 2, 7)
-        early = sb.tile([P, last, Q], F32, name="early", tag="ring%d" % last)
-        nc.scalar.copy(early[:, :, :P], result[0][:, : last * P].rearrange("p (j q) -> p j q", j=last))
-        nc.scalar.copy(early[:, :, P:], result[1][:, : last * P].rearrange("p (j q) -> p j q", j=last))
-        nc.sync.dma_start(out_rows[:, :last, :], early[:])
+        y = sb.tile([P, PACK, Q], F32, name="y", tag="ring%d" % last, align_bytes=64)
+        for j in range(last):
+            nc.vector.tensor_copy(y[:, j, :], results[j][:, :Q])
+        nc.sync.dma_start(out_rows[:, :last, :], y[:, :last, :])
 
-        multiply(last)
+        nc.scalar.copy(y[:, last, :], multiply(last, 6)[:, :Q])
+        nc.sync.dma_start(out_rows[:, last, :], y[:, last, :])
         y_grouped = sb.tile([P, Q, PACK], BF16, name="y_grouped", align_bytes=64)
-        nc.vector.tensor_copy(y_grouped[:, :P, :], result[0][:].rearrange("p (j q) -> p q j", j=PACK))
-        nc.scalar.copy(y_grouped[:, P:, :], result[1][:].rearrange("p (j q) -> p q j", j=PACK))
-        late = sb.tile([P, Q], F32, name="late")
-        for h in range(HALVES):
-            nc.scalar.copy(late[:, h * P : (h + 1) * P], result[h][:, last * P :])
-        nc.scalar.dma_start(out_rows[:, last, :], late[:])
+        for copy, cols in ((nc.vector.tensor_copy, slice(0, Y_SPLIT)), (nc.scalar.copy, slice(Y_SPLIT, Q))):
+            copy(
+                y_grouped[:, cols, :].rearrange("p (c i) j -> p c j i", i=4),
+                y[:, :, cols].rearrange("p j (c i) -> p c j i", i=4),
+            )
 
         y_codes, y_scales = mx_tiles("y", Q)
         nc.vector.quantize_mx(y_codes[:].bitcast(FP8X4), y_scales[:], y_grouped[:].rearrange("p q j -> p (q j)"))

@@ -66,16 +66,17 @@ def tile_attend_bothquestions_pl_kernel(
             return bias
 
         def load_query(n, src):
-            raw = sb.tile([P, PACK, Q], F32, name="q_raw%d" % n, tag=("ring0", "sig00")[n], align_bytes=64)
+            raw = sb.tile([P, PACK, Q], F32, name="q_raw%d" % n, tag="ring%d" % (2 * n), align_bytes=64)
             nc.sync.dma_start(raw[:], src.rearrange("(p j) q -> p j q", j=PACK))
             return raw
 
-        size_cols = sb.tile([P, PACK], F32, name="size_cols")
+        size_cols = sb.tile([P, PACK], F32, name="size_cols", tag="picked0", align_bytes=64)
         nc.sync.dma_start(size_cols[:], size.rearrange("o (p t) -> p (o t)", t=PACK))
-        biases = [load_bias(0, ba), load_bias(1, bb)]
+        biases = [load_bias(0, ba)]
         q_raw = [load_query(0, query)]
         key_word_pool = sb.tile([P, T], U16, name="key_word_pool")
         nc.sync.dma_start(key_word_pool[:].bitcast(I32), keys_words[0].bitcast(I32))
+        biases.append(load_bias(1, bb))
         q_raw.append(load_query(1, query2))
 
         vals_rows = vals.rearrange("(m j) t -> j m t", j=PACK)
@@ -105,21 +106,21 @@ def tile_attend_bothquestions_pl_kernel(
         sig = {}
         q_mx = [mx_tiles("q0", Q, "ring3"), mx_tiles("q1", Q)]
 
-        def quantise_query(n, cols, copy, tag):
-            width = cols.stop - cols.start
-            grouped = sb.tile([P, width, PACK], BF16, name="q_grouped_" + tag, tag=tag, align_bytes=64)
-            copy(
-                grouped[:].rearrange("p (c i) j -> p c j i", i=4),
-                q_raw[n][:, :, cols].rearrange("p j (c i) -> p c j i", i=4),
-            )
+        def quantise_query(n, copy, parts, tag):
+            grouped = sb.tile([P, Q, PACK], BF16, name="q_grouped%d" % n, tag=tag, align_bytes=64)
             codes, scales = q_mx[n]
-            nc.vector.quantize_mx(
-                codes[:, cols].bitcast(FP8X4), scales[:, cols], grouped[:].rearrange("p q j -> p (q j)")
-            )
+            for part in range(parts):
+                cols = slice(part * Q // parts, (part + 1) * Q // parts)
+                copy(
+                    grouped[:, cols, :].rearrange("p (c i) j -> p c j i", i=4),
+                    q_raw[n][:, :, cols].rearrange("p j (c i) -> p c j i", i=4),
+                )
+                nc.vector.quantize_mx(
+                    codes[:, cols].bitcast(FP8X4), scales[:, cols], grouped[:, cols, :].rearrange("p q j -> p (q j)")
+                )
 
-        quantise_query(0, slice(0, Q), nc.vector.tensor_copy, "ring1")
-        quantise_query(1, slice(0, P), nc.scalar.copy, "ring2")
-        quantise_query(1, slice(P, Q), nc.scalar.copy, "picked0")
+        quantise_query(0, nc.vector.tensor_copy, 1, "ring1")
+        quantise_query(1, nc.scalar.copy, HALVES, "picked0")
         for h in range(HALVES):
             cols = slice(h * P, (h + 1) * P)
             for n in range(2):
@@ -134,7 +135,7 @@ def tile_attend_bothquestions_pl_kernel(
                     start=True,
                     stop=True,
                 )
-                sig[n, h] = sb.tile([P, I], F32, name="sig%d%d" % (n, h), tag="sig%d%d" % (n, h), align_bytes=64)
+                sig[n, h] = sb.tile([P, I], F32, name="sig%d%d" % (n, h))
                 nc.scalar.activation(sig[n, h][:], scores[:], SIGMOID, bias=biases[n][:, h : h + 1])
 
         for j in range(PACK):

from contextlib import ExitStack

import concourse.mybir as mybir
from concourse.masks import make_identity

D, T, I, Q, E = 512, 2048, 512, 256, 512
FLOPS = 2 * D * Q * I * 2 + 2 * I * E * Q

F32 = mybir.dt.float32
BF16 = mybir.dt.bfloat16
I32 = mybir.dt.int32
U32 = mybir.dt.uint32
U16 = mybir.dt.uint16
U8 = mybir.dt.uint8
FP8X4 = mybir.dt.float8_e4m3fn_x4
FP4X4 = mybir.dt.float4_e2m1fn_x4
MULT = mybir.AluOpType.mult
COPY = mybir.ActivationFunctionType.Copy
SIGMOID = mybir.ActivationFunctionType.Sigmoid

P = 128
PACK = 4
HALVES = Q // P
BANK = 512
Y_SPLIT = 168


def tile_attend_bothquestions_pl_kernel(
    tc, query, query2, keys_words, keys_scales, ba, bb, size, vals, offs, out_0, out_1, out_2
):
    nc = tc.nc
    with ExitStack() as ctx:
        sb = ctx.enter_context(tc.tile_pool(name="sb", bufs=1))
        psum = ctx.enter_context(tc.psum_pool(name="psum", bufs=1))

        def bank(k, name):
            return psum.tile([P, BANK], F32, name=name, tag="bank%d" % k)

        def mx_tiles(name, width, tag=None):
            codes = sb.tile([P, width], U32, name=name + "_codes", tag=tag or name + "_codes", align_bytes=64)
            scales = sb.tile([P, width], U8, name=name + "_scales", align_bytes=64)
            return codes, scales

        offsets = sb.tile([P, I // 16], U16, name="offsets")
        nc.sync.dma_start(offsets[:], offs)

        warm_in = sb.tile([P, 1], F32, name="warm_in")
        warm_out = sb.tile([P, 1], F32, name="warm_out")
        nc.vector.memset(warm_in[:], 0.0)
        nc.scalar.activation(warm_out[:], warm_in[:], SIGMOID)

        key_scale_pool = sb.tile([P, T], U8, name="key_scale_pool")
        nc.vector.memset(key_scale_pool[:].bitcast(I32), 0)
        for quad in range(4):
            nc.scalar.dma_start(
                key_scale_pool[32 * quad : 32 * quad + 4, :].bitcast(I32),
                keys_scales[0, 4 * quad : 4 * quad + 4, :].bitcast(I32),
            )
        ident = sb.tile([P, P], F32, name="ident")
        make_identity(nc, ident[:])

        def load_bias(n, src):
            bias = sb.tile([P, HALVES], F32, name="bias%d" % n, tag=("bias0", "picked1")[n], align_bytes=64)
            with nc.allow_non_contiguous_dma(reason="one bias value a partition for each half of the query rows"):
                nc.sync.dma_start(bias[:], src.rearrange("(h p) o -> p (h o)", p=P))
            return bias

        def load_query(n, src):
            raw = sb.tile([P, PACK, Q], F32, name="q_raw%d" % n, tag="ring%d" % (2 * n), align_bytes=64)
            nc.sync.dma_start(raw[:], src.rearrange("(p j) q -> p j q", j=PACK))
            return raw

        size_cols = sb.tile([P, PACK], F32, name="size_cols", tag="picked0", align_bytes=64)
        nc.sync.dma_start(size_cols[:], size.rearrange("o (p t) -> p (o t)", t=PACK))
        biases = [load_bias(0, ba)]
        q_raw = [load_query(0, query)]
        key_word_pool = sb.tile([P, T], U16, name="key_word_pool")
        nc.sync.dma_start(key_word_pool[:].bitcast(I32), keys_words[0].bitcast(I32))
        biases.append(load_bias(1, bb))
        q_raw.append(load_query(1, query2))

        vals_rows = vals.rearrange("(m j) t -> j m t", j=PACK)
        val_pools = []

        def load_values(j):
            pool_j = sb.tile([P, T], F32, name="val_pool%d" % j, tag="ring%d" % j, align_bytes=64)
            nc.sync.dma_start(pool_j[:], vals_rows[j])
            val_pools.append(pool_j)

        key_words = sb.tile([P, I], U16, name="key_words", align_bytes=64)
        nc.vector.tensor_copy(key_words[:], key_word_pool[:].indirect(offsets[:]))

        key_scales = sb.tile([P, I], U8, name="key_scales", align_bytes=64)
        nc.vector.tensor_copy(key_scales[:], key_scale_pool[:].indirect(offsets[:]))

        size_bank = bank(3, "size_bank")
        for t in range(PACK):
            nc.tensor.transpose(
                size_bank[:, t * P : (t + 1) * P], size_cols[:, t : t + 1].to_broadcast([P, P]), ident[:]
            )
        size_rows = sb.tile([P, I], F32, name="size_rows")
        nc.scalar.copy(
            size_rows[:].rearrange("q (p t) -> q p t", t=PACK), size_bank[:].rearrange("q (t p) -> q p t", t=PACK)
        )

        sig = {}
        q_mx = [mx_tiles("q0", Q, "ring3"), mx_tiles("q1", Q)]

        def quantise_query(n, copy, parts, tag):
            grouped = sb.tile([P, Q, PACK], BF16, name="q_grouped%d" % n, tag=tag, align_bytes=64)
            codes, scales = q_mx[n]
            for part in range(parts):
                cols = slice(part * Q // parts, (part + 1) * Q // parts)
                copy(
                    grouped[:, cols, :].rearrange("p (c i) j -> p c j i", i=4),
                    q_raw[n][:, :, cols].rearrange("p j (c i) -> p c j i", i=4),
                )
                nc.vector.quantize_mx(
                    codes[:, cols].bitcast(FP8X4), scales[:, cols], grouped[:, cols, :].rearrange("p q j -> p (q j)")
                )

        quantise_query(0, nc.vector.tensor_copy, 1, "ring1")
        quantise_query(1, nc.scalar.copy, HALVES, "picked0")
        for h in range(HALVES):
            cols = slice(h * P, (h + 1) * P)
            for n in range(2):
                codes, scales = q_mx[n]
                scores = bank(3 + n, "scores%d%d" % (n, h))
                nc.tensor.matmul_mx(
                    scores[:],
                    lhsT=codes[:, cols].bitcast(FP8X4),
                    lhsT_scale=scales[:, cols],
                    rhs=key_words[:].bitcast(FP4X4),
                    rhs_scale=key_scales[:],
                    start=True,
                    stop=True,
                )
                sig[n, h] = sb.tile([P, I], F32, name="sig%d%d" % (n, h))
                nc.scalar.activation(sig[n, h][:], scores[:], SIGMOID, bias=biases[n][:, h : h + 1])

        for j in range(PACK):
            load_values(j)

        def turn_and_quantise(name, rows, turn_bank, codes, scales):
            words = rows[:].bitcast(F32)
            turned = bank(turn_bank, name + "_turned")
            for u in range(2):
                nc.tensor.transpose(turned[:, u * P : (u + 1) * P], words[:, u : I // 2 : 2], ident[:])
            grouped = sb.tile([P, P * PACK], BF16, name=name + "_grouped", tag=name + "_grouped", align_bytes=64)
            nc.scalar.copy(
                grouped[:].bitcast(F32).rearrange("p (c u) -> p c u", u=2),
                turned[:, : 2 * P].rearrange("p (u c) -> p c u", u=2),
            )
            nc.vector.quantize_mx(codes.bitcast(FP8X4), scales, grouped[:])

        def values(j, on_vector, turn_bank):
            picked = sb.tile([P, I], BF16, name="picked%d" % j, tag="picked%d" % min(j, 2), align_bytes=64)
            if on_vector > 0:
                nc.vector.tensor_copy(picked[:, :on_vector], val_pools[j][:].indirect(offsets[:, : on_vector // 16]))
            if on_vector < I:
                nc.scalar.activation(picked[:, on_vector:], val_pools[j][:].indirect(offsets[:, on_vector // 16 :]), COPY)
            codes, scales = mx_tiles("v%d" % j, P)
            turn_and_quantise("v%d" % j, picked, turn_bank, codes[:], scales[:])
            return codes, scales

        w_codes, w_scales = mx_tiles("w", Q)

        def weights(h, turn_bank):
            p = sb.tile([P, I], F32, name="p%d" % h, tag=("p0", "picked2")[h], align_bytes=64)
            total = sb.tile([P, 1], F32, name="total%d" % h)
            nc.vector.scalar_tensor_tensor(p[:], sig[0, h][:], 1.0, sig[1, h][:], MULT, MULT, accum_out=total[:])
            inverse = sb.tile([P, 1], F32, name="inverse%d" % h)
            nc.vector.reciprocal(inverse[:], total[:])
            w = sb.tile([P, I], BF16, name="w%d" % h)
            nc.vector.scalar_tensor_tensor(w[:], p[:], inverse[:], size_rows[:], MULT, MULT)
            cols = slice(h * P, (h + 1) * P)
            turn_and_quantise("w%d" % h, w, turn_bank, w_codes[:, cols], w_scales[:, cols])
            return w

        v_mx = {0: values(0, I, 7)}
        w_mx = [weights(0, 5), weights(1, 3)]
        v_mx[1] = values(1, 0, 6)
        v_mx[2] = values(2, I // 2, 4)

        def multiply(j, result_bank):
            result = bank(result_bank, "result%d" % j)
            nc.tensor.matmul_mx(
                result[:, :Q],
                lhsT=v_mx[j][0][:].bitcast(FP8X4),
                lhsT_scale=v_mx[j][1][:],
                rhs=w_codes[:].bitcast(FP8X4),
                rhs_scale=w_scales[:],
                start=True,
                stop=True,
            )
            return result

        out_rows = out_0.rearrange("(p j) q -> p j q", j=PACK)
        last = PACK - 1
        results = [multiply(j, j) for j in range(last)]
        v_mx[last] = values(last, I // 2, 7)
        y = sb.tile([P, PACK, Q], F32, name="y", tag="ring%d" % last, align_bytes=64)
        for j in range(last):
            nc.vector.tensor_copy(y[:, j, :], results[j][:, :Q])
        nc.sync.dma_start(out_rows[:, :last, :], y[:, :last, :])

        nc.scalar.copy(y[:, last, :], multiply(last, 6)[:, :Q])
        nc.sync.dma_start(out_rows[:, last, :], y[:, last, :])
        y_grouped = sb.tile([P, Q, PACK], BF16, name="y_grouped", align_bytes=64)
        for copy, cols in ((nc.vector.tensor_copy, slice(0, Y_SPLIT)), (nc.scalar.copy, slice(Y_SPLIT, Q))):
            copy(
                y_grouped[:, cols, :].rearrange("p (c i) j -> p c j i", i=4),
                y[:, :, cols].rearrange("p j (c i) -> p c j i", i=4),
            )

        y_codes, y_scales = mx_tiles("y", Q)
        nc.vector.quantize_mx(y_codes[:].bitcast(FP8X4), y_scales[:], y_grouped[:].rearrange("p q j -> p (q j)"))
        nc.sync.dma_start(out_1[0].rearrange("p c r -> p (c r)").bitcast(I32), y_codes[:].bitcast(I32))
        for quad in range(4):
            queue = nc.sync if quad % 2 == 0 else nc.scalar
            queue.dma_start(
                out_2[0, 4 * quad : 4 * quad + 4, :].bitcast(I32),
                y_scales[32 * quad : 32 * quad + 4, :].bitcast(I32),
            )
